import numpy as np
import ml_dtypes


def mxq(x, axis, fmt="e4m3"):
    dtype, down = {"e4m3": (ml_dtypes.float8_e4m3fn, 7), "e5m2": (ml_dtypes.float8_e5m2, 14)}[fmt]
    v = np.moveaxis(np.asarray(x, np.float32).astype(ml_dtypes.bfloat16).astype(np.float64), axis, -1)
    blocks = v.reshape(v.shape[:-1] + (-1, 32))
    amax = np.abs(blocks).max(-1, keepdims=True)
    byte = np.maximum(np.where(amax > 0, np.frexp(amax)[1] - 1 + 127, 0) - down, 1)
    scale = np.exp2(byte - 127.0)
    codes = (blocks / scale).astype(np.float32).astype(dtype).astype(np.float64)
    return np.moveaxis((codes * scale).reshape(v.shape), -1, axis)


WIDE = False


def mx_kscale(k):
    if not WIDE:
        return np.ones(k)
    levels = np.array([18, -18])
    if k % 512:
        return np.exp2(np.random.permutation(np.resize(levels, k // 32))).repeat(32)
    a = np.empty((k // 512, 16))
    for p in range(k // 512):
        a[p, :8] = np.random.permutation(np.resize(levels, 8))
        for g in range(8):
            far = levels[np.abs(levels - a[p, g]) >= 10]
            a[p, g + 8] = far[np.random.randint(len(far))]
    return np.exp2(a.ravel()).repeat(32)


def f64(x):
    return np.asarray(x).astype(np.float64)


def striped(idx):
    return np.tile(np.asarray(idx).reshape(-1, 16).T, (8, 1)).astype(np.uint16)


def unstriped(offs):
    return offs[:16].T.reshape(-1).astype(np.int64)


B, N, T, D, R = 1, 512, 2048, 512, 512


def setup_inputs():
    n = np.random.standard_normal
    idx = np.random.permutation(T)[:B * N]
    u = np.ones(T)
    u[idx] = mx_kscale(B * N)
    us = u[idx].reshape(B, N)
    z = mx_kscale(R)[:, None]
    act = n((B, R, N))
    s = mx_kscale(D)
    return {
        "zT": (act.transpose(0, 2, 1) * us[:, :, None]).astype(np.float32),
        "wT": (n((D, T)) / np.sqrt(N) / u * s[:, None]).astype(np.float32),
        "xm": (n((B, R, D)) * s).astype(np.float32),
        "wt": (np.random.uniform(0.5, 1.5, (B, R, 1)) / np.sqrt(R) * z).astype(np.float32),
        "zm": (act / z).astype(np.float32),
        "cs": np.tile(np.random.uniform(0.5, 1.5, D) / s, (128, 1)).astype(np.float32),
        "offs": striped(idx),
    }


def reference(zT, wT, xm, wt, zm, cs, offs):
    idx = unstriped(offs)
    pick = lambda x: x[:, idx].reshape(x.shape[0], B, N).transpose(1, 0, 2)
    w = pick(f64(wT))
    rec = mxq(f64(zT), 1, "e4m3").transpose(0, 2, 1) @ mxq(w, 2, "e4m3").transpose(0, 2, 1)
    q = f64(cs)[:1] * (rec - f64(xm))
    e = f64(wt) * f64(cs)[:1] * q
    dw = mxq(e, 1, "e5m2").transpose(0, 2, 1) @ mxq(f64(zm), 1, "e4m3")
    gw = np.zeros((D, T))
    gw[:, idx] = dw.transpose(1, 0, 2).reshape(D, B * N)
    gz = mxq(e, 2, "e5m2") @ mxq(w, 1, "e4m3")
    return gw, gz

@@ -1,0 +1,227 @@
+from contextlib import ExitStack
+
+import concourse.mybir as mybir
+from concourse.masks import make_identity
+
+N, T, D, R = 512, 2048, 512, 512
+P = 128
+FLOPS = 3 * 2 * N * D * R
+
+F32 = mybir.dt.float32
+BF16 = mybir.dt.bfloat16
+U32 = mybir.dt.uint32
+U16 = mybir.dt.uint16
+U8 = mybir.dt.uint8
+E4 = mybir.dt.float8_e4m3fn_x4
+E5 = mybir.dt.float8_e5m2_x4
+MULT = mybir.AluOpType.mult
+SUB = mybir.AluOpType.subtract
+
+
+def tile_attend_gdi_wz_kernel(tc, zT, wT, xm, wt, zm, cs, offs, out_0, out_1):
+    nc = tc.nc
+    with ExitStack() as ctx:
+        lists = ctx.enter_context(tc.tile_pool(name="lists", bufs=1))
+        sb = ctx.enter_context(tc.tile_pool(name="sb", bufs=1))
+        ps = ctx.enter_context(tc.psum_pool(name="ps", bufs=1))
+
+        def tile(name, width, dtype):
+            return sb.tile([P, width], dtype, name=name, align_bytes=64)
+
+        def bank(name, tag, bufs):
+            return ps.tile([P, 512], F32, name=name, tag=tag, bufs=bufs)
+
+        def quantize(name, src, fmt):
+            words = src.shape[1] // 4
+            codes = tile(name + "_codes", words, U32)
+            scales = tile(name + "_scales", words, U8)
+            nc.vector.quantize_mx(out=codes[:].bitcast(fmt), scales=scales[:], in_=src)
+            return codes, scales
+
+        offsets = lists.tile([P, N // 16], U16, name="offsets")
+        cs_col = tile("cs_col", 4, F32)
+        wt_col = tile("wt_col", 4, F32)
+        zT_raw = sb.tile([P, 4, R], F32, name="zT_raw")
+        xm_raw = sb.tile([P, 4, D], F32, name="xm_raw")
+        zm_raw = [sb.tile([P, 4, N // 2], F32, name="zm_raw%d" % h) for h in range(2)]
+        table = [tile("table%d" % t, T, F32) for t in range(4)]
+        wT_planes = wT.rearrange("(p t) c -> p t c", t=4)
+        zm_rows = zm[0].rearrange("(p j) i -> p j i", j=4)
+        nc.sync.dma_start(cs_col[:], cs[0:1, :].rearrange("o (q t) -> (o q) t", t=4))
+        nc.sync.dma_start(wt_col[:], wt[0].rearrange("(p j) o -> p (j o)", j=4))
+        nc.sync.dma_start(zT_raw[:], zT[0].rearrange("(p j) r -> p j r", j=4))
+        nc.sync.dma_start(offsets[:], offs)
+        nc.sync.dma_start(table[0][:], wT_planes[:, 0, :])
+        nc.sync.dma_start(table[1][:], wT_planes[:, 1, :])
+        nc.sync.dma_start(xm_raw[:], xm[0].rearrange("(p j) d -> p j d", j=4))
+        nc.sync.dma_start(table[2][:], wT_planes[:, 2, :])
+        nc.sync.dma_start(table[3][:], wT_planes[:, 3, :])
+        for h in range(2):
+            nc.sync.dma_start(zm_raw[h][:], zm_rows[:, :, h * 256 : (h + 1) * 256])
+
+        ident = tile("ident", P, F32)
+        make_identity(nc, ident[:])
+
+        window = [tile("window%d" % t, T, F32) for t in range(2)]
+        cs2_col = tile("cs2_col", 4, F32)
+        nc.vector.tensor_tensor(cs2_col[:], cs_col[:], cs_col[:], MULT)
+        for t in range(2):
+            nc.gpsimd.memset(window[t][:], 0.0)
+        cs2_rows = bank("cs2_rows", "turn", 2)
+        for t in range(4):
+            nc.tensor.transpose(cs2_rows[:, t * P : (t + 1) * P], cs2_col[:, t : t + 1].to_broadcast([P, P]), ident[:])
+        gain = tile("gain", 4 * D, F32)
+        nc.vector.tensor_tensor(
+            gain[:].rearrange("p (c j) -> p c j", j=4),
+            cs2_rows[:].unsqueeze(2).to_broadcast([P, D, 4]),
+            wt_col[:].unsqueeze(1).to_broadcast([P, D, 4]),
+            MULT,
+        )
+
+        zT_in = tile("zT_in", 4 * R, BF16)
+        nc.scalar.copy(
+            zT_in[:].rearrange("p (a m j) -> p m j a", a=4, j=4),
+            zT_raw[:].rearrange("p j (m a) -> p m j a", a=4),
+        )
+        zT_codes, zT_scales = quantize("zT", zT_in[:], E4)
+
+        picked = tile("picked", 4 * N, BF16)
+        rec = {}
+
+        def front(t):
+            nc.vector.tensor_copy(picked[:, t * N : (t + 1) * N], table[t][:].indirect(offsets[:]))
+            words = picked[:, t * N : (t + 1) * N].bitcast(F32)
+            turned = bank("w_turned%d" % t, "turn", 2)
+            for u in range(2):
+                nc.tensor.transpose(turned[:, u * P : (u + 1) * P], words[:, u : N // 2 : 2], ident[:])
+            wi_in = tile("wi_in%d" % t, 4 * P, BF16)
+            nc.scalar.copy(
+                wi_in[:].bitcast(F32).rearrange("p (q u) -> p q u", u=2),
+                turned[:, 0 : 2 * P].rearrange("p (u q) -> p q u", u=2),
+            )
+            codes, scales = quantize("wi%d" % t, wi_in[:], E4)
+            rec[t] = bank("rec%d" % t, "rec", 2)
+            for a in range(4):
+                nc.tensor.matmul_mx(
+                    rec[t][:, a * P : (a + 1) * P],
+                    lhsT=zT_codes[:, a * P : (a + 1) * P].bitcast(E4),
+                    lhsT_scale=zT_scales[:, a * P : (a + 1) * P],
+                    rhs=codes[:].bitcast(E4),
+                    rhs_scale=scales[:],
+                    start=True,
+                    stop=True,
+                )
+
+        xm_dealt = tile("xm_dealt", 4 * D, F32)
+        e_turned = [bank("e_turned%d" % u, "eturn%d" % u, 1) for u in range(2)]
+        resid = {}
+        e_r = {}
+        e_q = {}
+
+        def residual(t):
+            resid[t] = tile("resid%d" % t, D, F32)
+            nc.vector.tensor_tensor(
+                resid[t][:].rearrange("p (q a) -> p q a", a=4),
+                rec[t][:].rearrange("p (a q) -> p q a", a=4),
+                xm_dealt[:, t * D : (t + 1) * D].rearrange("p (q a) -> p q a", a=4),
+                SUB,
+            )
+
+        def weigh(t):
+            e_r[t] = tile("e_r%d" % t, D, BF16)
+            nc.vector.tensor_tensor(e_r[t][:], resid[t][:], gain[:, t * D : (t + 1) * D], MULT)
+
+        def quantize_e(t):
+            e_q[t] = quantize("er%d" % t, e_r[t][:], E5)
+            words = e_r[t][:].bitcast(F32)
+            for u in range(2):
+                nc.tensor.transpose(e_turned[u][:, t * P : (t + 1) * P], words[:, u : D // 2 : 2], ident[:])
+
+        front(0)
+        front(1)
+        dst = xm_dealt[:].rearrange("p (t q j) -> p q j t", t=4, j=4)
+        src = xm_raw[:].rearrange("p j (q t) -> p q j t", t=4)
+        nc.vector.tensor_copy(dst[:, 0:64], src[:, 0:64])
+        nc.scalar.copy(dst[:, 64:128], src[:, 64:128])
+        residual(0)
+        residual(1)
+        weigh(0)
+        weigh(1)
+        quantize_e(0)
+        quantize_e(1)
+        front(2)
+        front(3)
+        residual(2)
+        residual(3)
+        weigh(2)
+        weigh(3)
+        quantize_e(2)
+        quantize_e(3)
+
+        zm_codes = tile("zm_codes", N, U32)
+        zm_scales = tile("zm_scales", N, U8)
+        for h in range(2):
+            zm_in = tile("zm_in%d" % h, 2 * N, BF16)
+            nc.scalar.copy(
+                zm_in[:].rearrange("p (c i j) -> p c j i", i=4, j=4),
+                zm_raw[h][:].rearrange("p j (c i) -> p c j i", i=4),
+            )
+            cols = slice(h * 256, (h + 1) * 256)
+            nc.vector.quantize_mx(out=zm_codes[:, cols].bitcast(E4), scales=zm_scales[:, cols], in_=zm_in[:])
+
+        out0_planes = out_0.rearrange("(p t) c -> p t c", t=4)
+
+        def atoms_gradient(t, tag, bufs):
+            acc = bank("dw_acc%d" % t, tag, bufs)
+            nc.tensor.matmul_mx(
+                acc[:],
+                lhsT=e_q[t][0][:].bitcast(E5),
+                lhsT_scale=e_q[t][1][:],
+                rhs=zm_codes[:].bitcast(E4),
+                rhs_scale=zm_scales[:],
+                start=True,
+                stop=True,
+            )
+            dw = tile("dw%d" % t, N, F32)
+            nc.scalar.copy(dw[:], acc[:])
+            nc.vector.tensor_copy(window[t % 2][:].indirect(offsets[:]), dw[:])
+            nc.sync.dma_start(out0_planes[:, t, :], window[t % 2][:])
+
+        atoms_gradient(0, "dw", 2)
+        atoms_gradient(1, "dw", 2)
+
+        wd_in = tile("wd_in", 4 * N, BF16)
+        dst = wd_in[:].rearrange("p (c i t) -> p c t i", i=4, t=4)
+        src = picked[:].rearrange("p (t c i) -> p c t i", t=4, i=4)
+        for k in range(4):
+            nc.scalar.copy(dst[:, k * 32 : (k + 1) * 32], src[:, k * 32 : (k + 1) * 32])
+        wd_codes, wd_scales = quantize("wd", wd_in[:], E4)
+
+        ed = []
+        for u in range(2):
+            ed_in = tile("ed_in%d" % u, 2 * R, BF16)
+            nc.scalar.copy(
+                ed_in[:].rearrange("q (e p t) -> q e p t", e=2, t=4),
+                e_turned[u][:].bitcast(BF16).rearrange("q (t p e) -> q e p t", t=4, e=2),
+            )
+            ed.append(quantize("ed%d" % u, ed_in[:], E5))
+
+        atoms_gradient(2, "eturn0", 1)
+        atoms_gradient(3, "eturn1", 1)
+
+        out1_rows = out_1[0].rearrange("(p j) i -> p j i", j=4)
+        for u in range(2):
+            gz = tile("gz%d" % u, 2 * N, F32)
+            for e in range(2):
+                acc = bank("gz_acc%d%d" % (u, e), "rec" if u == 0 else "turn", 2)
+                nc.tensor.matmul_mx(
+                    acc[:],
+                    lhsT=ed[u][0][:, e * P : (e + 1) * P].bitcast(E5),
+                    lhsT_scale=ed[u][1][:, e * P : (e + 1) * P],
+                    rhs=wd_codes[:].bitcast(E4),
+                    rhs_scale=wd_scales[:],
+                    start=True,
+                    stop=True,
+                )
+                nc.scalar.copy(gz[:, e * N : (e + 1) * N], acc[:])
+            nc.scalar.dma_start(out1_rows[:, 2 * u : 2 * u + 2, :], gz[:].rearrange("p (e i) -> p e i", e=2))

@@ -1,7 +1,6 @@
 from contextlib import ExitStack
 
 import concourse.mybir as mybir
-from concourse.masks import make_identity
 
 N, T, D, R = 512, 2048, 512, 512
 P = 128
@@ -16,6 +15,7 @@ E4 = mybir.dt.float8_e4m3fn_x4
 E5 = mybir.dt.float8_e5m2_x4
 MULT = mybir.AluOpType.mult
 SUB = mybir.AluOpType.subtract
+SQUARE = mybir.ActivationFunctionType.Square
 
 
 def tile_attend_gdi_wz_kernel(tc, zT, wT, xm, wt, zm, cs, offs, out_0, out_1):
@@ -25,11 +25,10 @@ def tile_attend_gdi_wz_kernel(tc, zT, wT, xm, wt, zm, cs, offs, out_0, out_1):
         sb = ctx.enter_context(tc.tile_pool(name="sb", bufs=1))
         ps = ctx.enter_context(tc.psum_pool(name="ps", bufs=1))
 
-        def tile(name, width, dtype):
-            return sb.tile([P, width], dtype, name=name, align_bytes=64)
+        def tile(name, width, dtype, tag=""):
+            return sb.tile([P, width], dtype, name=name, tag=tag or name, align_bytes=64)
 
-        def bank(name, tag, bufs):
-            return ps.tile([P, 512], F32, name=name, tag=tag, bufs=bufs)
+        banks = [ps.tile([P, 512], F32, name="bank%d" % b) for b in range(8)]
 
         def quantize(name, src, fmt):
             words = src.shape[1] // 4
@@ -38,190 +37,265 @@ def tile_attend_gdi_wz_kernel(tc, zT, wT, xm, wt, zm, cs, offs, out_0, out_1):
             nc.vector.quantize_mx(out=codes[:].bitcast(fmt), scales=scales[:], in_=src)
             return codes, scales
 
+        def product(acc, lhs, lhs_fmt, cols, rhs):
+            nc.tensor.matmul_mx(
+                acc,
+                lhsT=lhs[0][:, cols].bitcast(lhs_fmt),
+                lhsT_scale=lhs[1][:, cols],
+                rhs=rhs[0][:].bitcast(E4),
+                rhs_scale=rhs[1][:],
+                start=True,
+                stop=True,
+            )
+
         offsets = lists.tile([P, N // 16], U16, name="offsets")
         cs_col = tile("cs_col", 4, F32)
         wt_col = tile("wt_col", 4, F32)
-        zT_raw = sb.tile([P, 4, R], F32, name="zT_raw")
-        xm_raw = sb.tile([P, 4, D], F32, name="xm_raw")
-        zm_raw = [sb.tile([P, 4, N // 2], F32, name="zm_raw%d" % h) for h in range(2)]
+        zT_raw = tile("zT_raw", 4 * R, F32)
+        xm_raw = tile("xm_raw", 4 * D, F32)
+        zm_raw = [tile("zm_raw%d" % h, 2 * N, F32) for h in range(2)]
         table = [tile("table%d" % t, T, F32) for t in range(4)]
         wT_planes = wT.rearrange("(p t) c -> p t c", t=4)
         zm_rows = zm[0].rearrange("(p j) i -> p j i", j=4)
+        out0_planes = out_0.rearrange("(p t) c -> p t c", t=4)
+        out1_rows = out_1[0].rearrange("(p j) i -> p j i", j=4)
+
+        def load_table(t):
+            nc.sync.dma_start(table[t][:], wT_planes[:, t, :])
+
+        def load_zm(h):
+            nc.sync.dma_start(zm_raw[h][:].rearrange("p (j i) -> p j i", j=4), zm_rows[:, :, h * 256 : (h + 1) * 256])
+
+        def load_zT():
+            nc.sync.dma_start(zT_raw[:], zT[0].rearrange("(p j) r -> p (j r)", j=4))
+
+        def load_xm():
+            nc.sync.dma_start(xm_raw[:], xm[0].rearrange("(p j) d -> p (j d)", j=4))
+
         nc.sync.dma_start(cs_col[:], cs[0:1, :].rearrange("o (q t) -> (o q) t", t=4))
         nc.sync.dma_start(wt_col[:], wt[0].rearrange("(p j) o -> p (j o)", j=4))
-        nc.sync.dma_start(zT_raw[:], zT[0].rearrange("(p j) r -> p j r", j=4))
+        load_table(0)
         nc.sync.dma_start(offsets[:], offs)
-        nc.sync.dma_start(table[0][:], wT_planes[:, 0, :])
-        nc.sync.dma_start(table[1][:], wT_planes[:, 1, :])
-        nc.sync.dma_start(xm_raw[:], xm[0].rearrange("(p j) d -> p j d", j=4))
-        nc.sync.dma_start(table[2][:], wT_planes[:, 2, :])
-        nc.sync.dma_start(table[3][:], wT_planes[:, 3, :])
-        for h in range(2):
-            nc.sync.dma_start(zm_raw[h][:], zm_rows[:, :, h * 256 : (h + 1) * 256])
+        load_table(1)
+        load_zT()
+        load_table(2)
+        load_table(3)
+        load_xm()
+        load_zm(0)
+        load_zm(1)
 
         ident = tile("ident", P, F32)
-        make_identity(nc, ident[:])
+        zeros = tile("zeros", P, F32, tag="window1")
+        nc.vector.memset(zeros[:], 0.0)
+        nc.gpsimd.affine_select(
+            out=ident[:], in_=zeros[:], compare_op=mybir.AluOpType.not_equal, fill=1.0, base=0,
+            pattern=[[-1, P]], channel_multiplier=1,
+        )
+        window = [tile("window0", T, F32), tile("window1", T, F32), tile("window2", T, F32, tag="cs_col")]
+        nc.vector.memset(window[0][:], 0.0)
+        nc.gpsimd.memset(window[1][:], 0.0)
 
-        window = [tile("window%d" % t, T, F32) for t in range(2)]
         cs2_col = tile("cs2_col", 4, F32)
-        nc.vector.tensor_tensor(cs2_col[:], cs_col[:], cs_col[:], MULT)
-        for t in range(2):
-            nc.gpsimd.memset(window[t][:], 0.0)
-        cs2_rows = bank("cs2_rows", "turn", 2)
+        nc.scalar.activation(cs2_col[:], cs_col[:], SQUARE)
+        nc.gpsimd.memset(window[2][:], 0.0)
         for t in range(4):
-            nc.tensor.transpose(cs2_rows[:, t * P : (t + 1) * P], cs2_col[:, t : t + 1].to_broadcast([P, P]), ident[:])
-        gain = tile("gain", 4 * D, F32)
-        nc.vector.tensor_tensor(
-            gain[:].rearrange("p (c j) -> p c j", j=4),
-            cs2_rows[:].unsqueeze(2).to_broadcast([P, D, 4]),
-            wt_col[:].unsqueeze(1).to_broadcast([P, D, 4]),
-            MULT,
-        )
+            nc.tensor.transpose(banks[7][:, t * P : (t + 1) * P], cs2_col[:, t : t + 1].to_broadcast([P, P]), ident[:])
+        zT_in = tile("zT_in", 4 * R, BF16)[:]
+        xm_dealt = tile("xm_dealt", 4 * D, F32)[:]
+        picked = tile("picked", 4 * N, BF16)[:]
+        zm_in = [tile("zm_in%d" % h, 2 * N, BF16)[:] for h in range(2)]
+        wi01_in = zT_raw[:, 0:N].bitcast(BF16)
+        wi23_in = xm_raw[:, 0:N].bitcast(BF16)
+        wi_in = [wi01_in[:, 0:N], wi01_in[:, N : 2 * N], wi23_in[:, 0:N], wi23_in[:, N : 2 * N]]
+        resid = [tile("resid%d" % t, D, F32)[:] for t in range(4)]
+        e_r = [tile("e_r%d" % t, D, BF16)[:] for t in range(4)]
+        dw = [tile("dw%d" % t, N, F32)[:] for t in range(4)]
+        wd_in = zm_raw[1][:].bitcast(BF16)
+        ed_in = [tile("ed_in%d" % u, 2 * R, BF16)[:] for u in range(2)]
+        w_bank = [0, 6, 0, 6]
+        rec_bank = [1, 2, 3, 7]
+        e_bank = [4, 5]
+        dw_bank = [1, 4, 5, 0]
+        gz_bank = [0, 2, 3, 7]
+        q = {}
 
-        zT_in = tile("zT_in", 4 * R, BF16)
-        nc.scalar.copy(
-            zT_in[:].rearrange("p (a m j) -> p m j a", a=4, j=4),
-            zT_raw[:].rearrange("p j (m a) -> p m j a", a=4),
-        )
-        zT_codes, zT_scales = quantize("zT", zT_in[:], E4)
+        def lay_zT(engine_copy, lo, hi):
+            engine_copy(
+                zT_in.rearrange("p (a m j) -> p m j a", a=4, j=4)[:, lo:hi],
+                zT_raw[:].rearrange("p (j m a) -> p m j a", j=4, a=4)[:, lo:hi],
+            )
 
-        picked = tile("picked", 4 * N, BF16)
-        rec = {}
+        def lay_xm(engine_copy, lo, hi):
+            engine_copy(
+                xm_dealt.rearrange("p (t q j) -> p q j t", t=4, j=4)[:, lo:hi],
+                xm_raw[:].rearrange("p (j q t) -> p q j t", j=4, t=4)[:, lo:hi],
+            )
 
-        def front(t):
+        def lay_zm(engine_copy, h):
+            engine_copy(
+                zm_in[h].rearrange("p (c i j) -> p c j i", i=4, j=4),
+                zm_raw[h][:].rearrange("p (j c i) -> p c j i", j=4, i=4),
+            )
+
+        zm_q = (tile("zm_codes", N, U32), tile("zm_scales", N, U8))
+
+        def quantize_zm(h):
+            cols = slice(h * 256, (h + 1) * 256)
+            nc.vector.quantize_mx(out=zm_q[0][:, cols].bitcast(E4), scales=zm_q[1][:, cols], in_=zm_in[h])
+
+        def gather(t):
             nc.vector.tensor_copy(picked[:, t * N : (t + 1) * N], table[t][:].indirect(offsets[:]))
+
+        def turn_w(t, engine_copy=nc.scalar.copy):
             words = picked[:, t * N : (t + 1) * N].bitcast(F32)
-            turned = bank("w_turned%d" % t, "turn", 2)
+            turned = banks[w_bank[t]]
             for u in range(2):
-                nc.tensor.transpose(turned[:, u * P : (u + 1) * P], words[:, u : N // 2 : 2], ident[:])
-            wi_in = tile("wi_in%d" % t, 4 * P, BF16)
-            nc.scalar.copy(
-                wi_in[:].bitcast(F32).rearrange("p (q u) -> p q u", u=2),
+                nc.tensor.transpose(turned[:, u * P : (u + 1) * P], words[:, u : 2 * P : 2], ident[:])
+            engine_copy(
+                wi_in[t].bitcast(F32).rearrange("p (q u) -> p q u", u=2),
                 turned[:, 0 : 2 * P].rearrange("p (u q) -> p q u", u=2),
             )
-            codes, scales = quantize("wi%d" % t, wi_in[:], E4)
-            rec[t] = bank("rec%d" % t, "rec", 2)
-            for a in range(4):
-                nc.tensor.matmul_mx(
-                    rec[t][:, a * P : (a + 1) * P],
-                    lhsT=zT_codes[:, a * P : (a + 1) * P].bitcast(E4),
-                    lhsT_scale=zT_scales[:, a * P : (a + 1) * P],
-                    rhs=codes[:].bitcast(E4),
-                    rhs_scale=scales[:],
-                    start=True,
-                    stop=True,
-                )
 
-        xm_dealt = tile("xm_dealt", 4 * D, F32)
-        e_turned = [bank("e_turned%d" % u, "eturn%d" % u, 1) for u in range(2)]
-        resid = {}
-        e_r = {}
-        e_q = {}
+        def quantize_w(t):
+            q["wi", t] = quantize("wi%d" % t, wi_in[t], E4)
+
+        def quantize_w01():
+            codes, scales = quantize("wi01", wi01_in, E4)
+            for t in range(2):
+                q["wi", t] = (codes[:, t * P : (t + 1) * P], scales[:, t * P : (t + 1) * P])
+
+        def quantize_w23():
+            codes, scales = quantize("wi23", wi23_in, E4)
+            for t in range(2):
+                q["wi", 2 + t] = (codes[:, t * P : (t + 1) * P], scales[:, t * P : (t + 1) * P])
+
+        def reconstruct(t):
+            wi_q = q["wi", t]
+            for a in range(4):
+                cols = slice(a * P, (a + 1) * P)
+                product(banks[rec_bank[t]][:, cols], q["zT"], E4, cols, wi_q)
 
         def residual(t):
-            resid[t] = tile("resid%d" % t, D, F32)
             nc.vector.tensor_tensor(
-                resid[t][:].rearrange("p (q a) -> p q a", a=4),
-                rec[t][:].rearrange("p (a q) -> p q a", a=4),
+                resid[t].rearrange("p (q a) -> p q a", a=4),
+                banks[rec_bank[t]][:].rearrange("p (a q) -> p q a", a=4),
                 xm_dealt[:, t * D : (t + 1) * D].rearrange("p (q a) -> p q a", a=4),
                 SUB,
             )
 
         def weigh(t):
-            e_r[t] = tile("e_r%d" % t, D, BF16)
-            nc.vector.tensor_tensor(e_r[t][:], resid[t][:], gain[:, t * D : (t + 1) * D], MULT)
+            nc.vector.tensor_tensor(e_r[t], resid[t], gain[:, t * D : (t + 1) * D], MULT)
 
         def quantize_e(t):
-            e_q[t] = quantize("er%d" % t, e_r[t][:], E5)
-            words = e_r[t][:].bitcast(F32)
-            for u in range(2):
-                nc.tensor.transpose(e_turned[u][:, t * P : (t + 1) * P], words[:, u : D // 2 : 2], ident[:])
+            q["e", t] = quantize("er%d" % t, e_r[t], E5)
 
-        front(0)
-        front(1)
-        dst = xm_dealt[:].rearrange("p (t q j) -> p q j t", t=4, j=4)
-        src = xm_raw[:].rearrange("p j (q t) -> p q j t", t=4)
-        nc.vector.tensor_copy(dst[:, 0:64], src[:, 0:64])
-        nc.scalar.copy(dst[:, 64:128], src[:, 64:128])
+        def turn_e(t):
+            words = e_r[t].bitcast(F32)
+            for u in range(2):
+                nc.tensor.transpose(banks[e_bank[u]][:, t * P : (t + 1) * P], words[:, u : 2 * P : 2], ident[:])
+
+        def atoms_product(t):
+            product(banks[dw_bank[t]][:], q["e", t], E5, slice(0, P), zm_q)
+
+        def leave(t, lo, hi):
+            nc.scalar.copy(dw[t][:, lo:hi], banks[dw_bank[t]][:, lo:hi])
+
+        def scatter(t, lo, hi):
+            win = window[t % len(window)]
+            nc.vector.tensor_copy(win[:].indirect(offsets[:, lo // 16 : hi // 16]), dw[t][:, lo:hi])
+            if hi == N:
+                nc.sync.dma_start(out0_planes[:, t, :], win[:])
+
+        def lay_wd(k):
+            nc.scalar.copy(
+                wd_in[:, k * N : (k + 1) * N].rearrange("p (c i t) -> p c t i", i=4, t=4),
+                picked.rearrange("p (t c i) -> p c t i", t=4, i=4)[:, k * 32 : (k + 1) * 32],
+            )
+
+        def lay_ed(u):
+            nc.scalar.copy(
+                ed_in[u].rearrange("q (e p t) -> q e p t", e=2, t=4),
+                banks[e_bank[u]][:].bitcast(BF16).rearrange("q (t p e) -> q e p t", t=4, e=2),
+            )
+
+        def quantize_ed(u):
+            q["ed", u] = quantize("ed%d" % u, ed_in[u], E5)
+
+        def codes_gradient(u):
+            gz = tile("gz%d" % u, 2 * N, F32)
+            for e in range(2):
+                acc = banks[gz_bank[2 * u + e]]
+                product(acc[:], q["ed", u], E5, slice(e * P, (e + 1) * P), q["wd"])
+                nc.scalar.copy(gz[:, e * N : (e + 1) * N], acc[:])
+            nc.scalar.dma_start(out1_rows[:, 2 * u : 2 * u + 2, :], gz[:].rearrange("p (e i) -> p e i", e=2))
+
+        gain = tile("gain", 4 * D, F32, tag="gain")
+        nc.vector.tensor_tensor(
+            gain[:].rearrange("p (c j) -> p c j", j=4),
+            banks[7][:].unsqueeze(2).to_broadcast([P, D, 4]),
+            wt_col[:].unsqueeze(1).to_broadcast([P, D, 4]),
+            MULT,
+        )
+
+        gather(0)
+        gather(1)
+        lay_zT(nc.vector.tensor_copy, 0, 80)
+        lay_zT(nc.scalar.copy, 80, 128)
+        turn_w(0)
+        turn_w(1)
+        q["zT"] = quantize("zT", zT_in, E4)
+        quantize_w01()
+        reconstruct(0)
+        reconstruct(1)
+        gather(2)
+        gather(3)
+        lay_xm(nc.vector.tensor_copy, 0, 80)
+        lay_xm(nc.scalar.copy, 80, 128)
+        turn_w(2)
+        turn_w(3)
+        quantize_w23()
+        reconstruct(2)
+        reconstruct(3)
+        lay_zm(nc.scalar.copy, 0)
+        quantize_zm(0)
+        lay_zm(nc.scalar.copy, 1)
+        quantize_zm(1)
         residual(0)
         residual(1)
         weigh(0)
         weigh(1)
         quantize_e(0)
+        turn_e(0)
         quantize_e(1)
-        front(2)
-        front(3)
+        turn_e(1)
         residual(2)
         residual(3)
         weigh(2)
         weigh(3)
         quantize_e(2)
+        turn_e(2)
         quantize_e(3)
-
-        zm_codes = tile("zm_codes", N, U32)
-        zm_scales = tile("zm_scales", N, U8)
-        for h in range(2):
-            zm_in = tile("zm_in%d" % h, 2 * N, BF16)
-            nc.scalar.copy(
-                zm_in[:].rearrange("p (c i j) -> p c j i", i=4, j=4),
-                zm_raw[h][:].rearrange("p j (c i) -> p c j i", i=4),
-            )
-            cols = slice(h * 256, (h + 1) * 256)
-            nc.vector.quantize_mx(out=zm_codes[:, cols].bitcast(E4), scales=zm_scales[:, cols], in_=zm_in[:])
-
-        out0_planes = out_0.rearrange("(p t) c -> p t c", t=4)
-
-        def atoms_gradient(t, tag, bufs):
-            acc = bank("dw_acc%d" % t, tag, bufs)
-            nc.tensor.matmul_mx(
-                acc[:],
-                lhsT=e_q[t][0][:].bitcast(E5),
-                lhsT_scale=e_q[t][1][:],
-                rhs=zm_codes[:].bitcast(E4),
-                rhs_scale=zm_scales[:],
-                start=True,
-                stop=True,
-            )
-            dw = tile("dw%d" % t, N, F32)
-            nc.scalar.copy(dw[:], acc[:])
-            nc.vector.tensor_copy(window[t % 2][:].indirect(offsets[:]), dw[:])
-            nc.sync.dma_start(out0_planes[:, t, :], window[t % 2][:])
-
-        atoms_gradient(0, "dw", 2)
-        atoms_gradient(1, "dw", 2)
-
-        wd_in = tile("wd_in", 4 * N, BF16)
-        dst = wd_in[:].rearrange("p (c i t) -> p c t i", i=4, t=4)
-        src = picked[:].rearrange("p (t c i) -> p c t i", t=4, i=4)
-        for k in range(4):
-            nc.scalar.copy(dst[:, k * 32 : (k + 1) * 32], src[:, k * 32 : (k + 1) * 32])
-        wd_codes, wd_scales = quantize("wd", wd_in[:], E4)
-
-        ed = []
-        for u in range(2):
-            ed_in = tile("ed_in%d" % u, 2 * R, BF16)
-            nc.scalar.copy(
-                ed_in[:].rearrange("q (e p t) -> q e p t", e=2, t=4),
-                e_turned[u][:].bitcast(BF16).rearrange("q (t p e) -> q e p t", t=4, e=2),
-            )
-            ed.append(quantize("ed%d" % u, ed_in[:], E5))
-
-        atoms_gradient(2, "eturn0", 1)
-        atoms_gradient(3, "eturn1", 1)
-
-        out1_rows = out_1[0].rearrange("(p j) i -> p j i", j=4)
-        for u in range(2):
-            gz = tile("gz%d" % u, 2 * N, F32)
-            for e in range(2):
-                acc = bank("gz_acc%d%d" % (u, e), "rec" if u == 0 else "turn", 2)
-                nc.tensor.matmul_mx(
-                    acc[:],
-                    lhsT=ed[u][0][:, e * P : (e + 1) * P].bitcast(E5),
-                    lhsT_scale=ed[u][1][:, e * P : (e + 1) * P],
-                    rhs=wd_codes[:].bitcast(E4),
-                    rhs_scale=wd_scales[:],
-                    start=True,
-                    stop=True,
-                )
-                nc.scalar.copy(gz[:, e * N : (e + 1) * N], acc[:])
-            nc.scalar.dma_start(out1_rows[:, 2 * u : 2 * u + 2, :], gz[:].rearrange("p (e i) -> p e i", e=2))
+        turn_e(3)
+        atoms_product(0)
+        leave(0, 0, 512)
+        scatter(0, 0, 512)
+        lay_wd(0)
+        lay_wd(1)
+        lay_wd(2)
+        lay_wd(3)
+        q["wd"] = quantize("wd", wd_in, E4)
+        lay_ed(0)
+        quantize_ed(0)
+        lay_ed(1)
+        quantize_ed(1)
+        atoms_product(1)
+        leave(1, 0, 512)
+        scatter(1, 0, 512)
+        codes_gradient(0)
+        atoms_product(2)
+        leave(2, 0, 512)
+        scatter(2, 0, 512)
+        codes_gradient(1)
+        atoms_product(3)
+        leave(3, 0, 512)
+        scatter(3, 0, 512)

@@ -72,8 +72,8 @@ def tile_attend_gdi_wz_kernel(tc, zT, wT, xm, wt, zm, cs, offs, out_0, out_1):
         def load_xm():
             nc.sync.dma_start(xm_raw[:], xm[0].rearrange("(p j) d -> p (j d)", j=4))
 
-        nc.sync.dma_start(cs_col[:], cs[0:1, :].rearrange("o (q t) -> (o q) t", t=4))
-        nc.sync.dma_start(wt_col[:], wt[0].rearrange("(p j) o -> p (j o)", j=4))
+        nc.scalar.dma_start(cs_col[:], cs[0:1, :].rearrange("o (q t) -> (o q) t", t=4))
+        nc.scalar.dma_start(wt_col[:], wt[0].rearrange("(p j) o -> p (j o)", j=4))
         load_table(0)
         nc.sync.dma_start(offsets[:], offs)
         load_table(1)
@@ -108,10 +108,12 @@ def tile_attend_gdi_wz_kernel(tc, zT, wT, xm, wt, zm, cs, offs, out_0, out_1):
         wi23_in = xm_raw[:, 0:N].bitcast(BF16)
         wi_in = [wi01_in[:, 0:N], wi01_in[:, N : 2 * N], wi23_in[:, 0:N], wi23_in[:, N : 2 * N]]
         resid = [tile("resid%d" % t, D, F32)[:] for t in range(4)]
-        e_r = [tile("e_r%d" % t, D, BF16)[:] for t in range(4)]
+        e_pair = [tile("e_pair%d" % k, 2 * D, BF16)[:] for k in range(2)]
+        e_r = [e_pair[t // 2][:, (t % 2) * D : (t % 2 + 1) * D] for t in range(4)]
         dw = [tile("dw%d" % t, N, F32)[:] for t in range(4)]
         wd_in = zm_raw[1][:].bitcast(BF16)
-        ed_in = [tile("ed_in%d" % u, 2 * R, BF16)[:] for u in range(2)]
+        ed_both = tile("ed_both", 4 * R, BF16)[:]
+        ed_in = [ed_both[:, u * 2 * R : (u + 1) * 2 * R] for u in range(2)]
         w_bank = [0, 6, 0, 6]
         rec_bank = [1, 2, 3, 7]
         e_bank = [4, 5]
@@ -183,11 +185,21 @@ def tile_attend_gdi_wz_kernel(tc, zT, wT, xm, wt, zm, cs, offs, out_0, out_1):
                 SUB,
             )
 
-        def weigh(t):
-            nc.vector.tensor_tensor(e_r[t], resid[t], gain[:, t * D : (t + 1) * D], MULT)
+        def weigh(t, engine=nc.vector):
+            engine.tensor_tensor(e_r[t], resid[t], gain[:, t * D : (t + 1) * D], MULT)
 
         def quantize_e(t):
             q["e", t] = quantize("er%d" % t, e_r[t], E5)
+
+        def quantize_e_pair(k):
+            codes, scales = quantize("er_pair%d" % k, e_pair[k], E5)
+            for t in range(2):
+                q["e", 2 * k + t] = (codes[:, t * P : (t + 1) * P], scales[:, t * P : (t + 1) * P])
+
+        def quantize_ed_both():
+            codes, scales = quantize("ed", ed_both, E5)
+            for u in range(2):
+                q["ed", u] = (codes[:, u * 256 : (u + 1) * 256], scales[:, u * 256 : (u + 1) * 256])
 
         def turn_e(t):
             words = e_r[t].bitcast(F32)
@@ -264,17 +276,15 @@ def tile_attend_gdi_wz_kernel(tc, zT, wT, xm, wt, zm, cs, offs, out_0, out_1):
         residual(1)
         weigh(0)
         weigh(1)
-        quantize_e(0)
+        quantize_e_pair(0)
         turn_e(0)
-        quantize_e(1)
         turn_e(1)
         residual(2)
         residual(3)
         weigh(2)
         weigh(3)
-        quantize_e(2)
+        quantize_e_pair(1)
         turn_e(2)
-        quantize_e(3)
         turn_e(3)
         atoms_product(0)
         leave(0, 0, 512)
@@ -285,9 +295,8 @@ def tile_attend_gdi_wz_kernel(tc, zT, wT, xm, wt, zm, cs, offs, out_0, out_1):
         lay_wd(3)
         q["wd"] = quantize("wd", wd_in, E4)
         lay_ed(0)
-        quantize_ed(0)
         lay_ed(1)
-        quantize_ed(1)
+        quantize_ed_both()
         atoms_product(1)
         leave(1, 0, 512)
         scatter(1, 0, 512)

@@ -4,17 +4,20 @@ import concourse.mybir as mybir
 
 N, T, D, R = 512, 2048, 512, 512
 P = 128
+PACK = 4
 FLOPS = 3 * 2 * N * D * R
+
+VECTOR_SHARE = 80
 
 F32 = mybir.dt.float32
 BF16 = mybir.dt.bfloat16
 U32 = mybir.dt.uint32
 U16 = mybir.dt.uint16
 U8 = mybir.dt.uint8
-E4 = mybir.dt.float8_e4m3fn_x4
-E5 = mybir.dt.float8_e5m2_x4
+E4M3 = mybir.dt.float8_e4m3fn_x4
+E5M2 = mybir.dt.float8_e5m2_x4
 MULT = mybir.AluOpType.mult
-SUB = mybir.AluOpType.subtract
+SUBTRACT = mybir.AluOpType.subtract
 SQUARE = mybir.ActivationFunctionType.Square
 
 
@@ -28,283 +31,202 @@ def tile_attend_gdi_wz_kernel(tc, zT, wT, xm, wt, zm, cs, offs, out_0, out_1):
         def tile(name, width, dtype, tag=""):
             return sb.tile([P, width], dtype, name=name, tag=tag or name, align_bytes=64)
 
-        banks = [ps.tile([P, 512], F32, name="bank%d" % b) for b in range(8)]
+        def part(ap, index, width):
+            return ap[:, index * width : (index + 1) * width]
 
-        def quantize(name, src, fmt):
-            words = src.shape[1] // 4
-            codes = tile(name + "_codes", words, U32)
-            scales = tile(name + "_scales", words, U8)
-            nc.vector.quantize_mx(out=codes[:].bitcast(fmt), scales=scales[:], in_=src)
-            return codes, scales
+        def quantize(name, values, fmt):
+            words = tile(name + "_words", values.shape[1] // PACK, U32)
+            scales = tile(name + "_scales", values.shape[1] // PACK, U8)
+            nc.vector.quantize_mx(out=words[:].bitcast(fmt), scales=scales[:], in_=values)
+            return words[:], scales[:]
 
-        def product(acc, lhs, lhs_fmt, cols, rhs):
+        def columns(operand, index, width):
+            return part(operand[0], index, width), part(operand[1], index, width)
+
+        def product(acc, stationary, stationary_fmt, moving):
             nc.tensor.matmul_mx(
                 acc,
-                lhsT=lhs[0][:, cols].bitcast(lhs_fmt),
-                lhsT_scale=lhs[1][:, cols],
-                rhs=rhs[0][:].bitcast(E4),
-                rhs_scale=rhs[1][:],
+                lhsT=stationary[0].bitcast(stationary_fmt),
+                lhsT_scale=stationary[1],
+                rhs=moving[0].bitcast(E4M3),
+                rhs_scale=moving[1],
                 start=True,
                 stop=True,
             )
 
+        banks = [ps.tile([P, 512], F32, name="bank%d" % b) for b in range(8)]
+        cs2_bank = banks[7]
+        w_turn_bank = [banks[0], banks[6], banks[0], banks[6]]
+        rec_bank = [banks[1], banks[2], banks[3], banks[7]]
+        e_turn_bank = [banks[4], banks[5]]
+        dw_bank = [banks[1], banks[4], banks[5], banks[0]]
+        dz_bank = [banks[0], banks[2], banks[3], banks[7]]
+
         offsets = lists.tile([P, N // 16], U16, name="offsets")
-        cs_col = tile("cs_col", 4, F32)
-        wt_col = tile("wt_col", 4, F32)
-        zT_raw = tile("zT_raw", 4 * R, F32)
-        xm_raw = tile("xm_raw", 4 * D, F32)
-        zm_raw = [tile("zm_raw%d" % h, 2 * N, F32) for h in range(2)]
-        table = [tile("table%d" % t, T, F32) for t in range(4)]
-        wT_planes = wT.rearrange("(p t) c -> p t c", t=4)
-        zm_rows = zm[0].rearrange("(p j) i -> p j i", j=4)
-        out0_planes = out_0.rearrange("(p t) c -> p t c", t=4)
-        out1_rows = out_1[0].rearrange("(p j) i -> p j i", j=4)
+        cs_col = tile("cs_col", PACK, F32)
+        wt_col = tile("wt_col", PACK, F32)
+        zT_raw = tile("zT_raw", PACK * R, F32)
+        xm_raw = tile("xm_raw", PACK * D, F32)
+        zm_raw = tile("zm_raw", PACK * N, F32)
+        table = [tile("table%d" % t, T, F32) for t in range(PACK)]
+        wT_planes = wT.rearrange("(q t) c -> q t c", t=PACK)
+        out_0_planes = out_0.rearrange("(q t) c -> q t c", t=PACK)
+        out_1_rows = out_1[0].rearrange("(m a) i -> m a i", a=PACK)
 
-        def load_table(t):
-            nc.sync.dma_start(table[t][:], wT_planes[:, t, :])
-
-        def load_zm(h):
-            nc.sync.dma_start(zm_raw[h][:].rearrange("p (j i) -> p j i", j=4), zm_rows[:, :, h * 256 : (h + 1) * 256])
-
-        def load_zT():
-            nc.sync.dma_start(zT_raw[:], zT[0].rearrange("(p j) r -> p (j r)", j=4))
-
-        def load_xm():
-            nc.sync.dma_start(xm_raw[:], xm[0].rearrange("(p j) d -> p (j d)", j=4))
-
-        nc.scalar.dma_start(cs_col[:], cs[0:1, :].rearrange("o (q t) -> (o q) t", t=4))
-        nc.scalar.dma_start(wt_col[:], wt[0].rearrange("(p j) o -> p (j o)", j=4))
-        load_table(0)
+        nc.sync.dma_start(cs_col[:], cs[0:1, :].rearrange("o (q t) -> (o q) t", t=PACK))
+        nc.sync.dma_start(wt_col[:], wt[0].rearrange("(m a) o -> m (a o)", a=PACK))
+        nc.sync.dma_start(table[0][:], wT_planes[:, 0, :])
         nc.sync.dma_start(offsets[:], offs)
-        load_table(1)
-        load_zT()
-        load_table(2)
-        load_table(3)
-        load_xm()
-        load_zm(0)
-        load_zm(1)
+        nc.sync.dma_start(table[1][:], wT_planes[:, 1, :])
+        nc.sync.dma_start(zT_raw[:], zT[0].rearrange("(p s) r -> p (s r)", s=PACK))
+        nc.sync.dma_start(table[2][:], wT_planes[:, 2, :])
+        nc.sync.dma_start(table[3][:], wT_planes[:, 3, :])
+        nc.sync.dma_start(xm_raw[:], xm[0].rearrange("(m a) d -> m (a d)", a=PACK))
+        nc.sync.dma_start(zm_raw[:], zm[0].rearrange("(m a) i -> m (a i)", a=PACK))
 
         ident = tile("ident", P, F32)
         zeros = tile("zeros", P, F32, tag="window1")
         nc.vector.memset(zeros[:], 0.0)
         nc.gpsimd.affine_select(
-            out=ident[:], in_=zeros[:], compare_op=mybir.AluOpType.not_equal, fill=1.0, base=0,
-            pattern=[[-1, P]], channel_multiplier=1,
+            out=ident[:],
+            in_=zeros[:],
+            compare_op=mybir.AluOpType.not_equal,
+            fill=1.0,
+            base=0,
+            pattern=[[-1, P]],
+            channel_multiplier=1,
         )
         window = [tile("window0", T, F32), tile("window1", T, F32), tile("window2", T, F32, tag="cs_col")]
         nc.vector.memset(window[0][:], 0.0)
         nc.gpsimd.memset(window[1][:], 0.0)
 
-        cs2_col = tile("cs2_col", 4, F32)
+        cs2_col = tile("cs2_col", PACK, F32)
         nc.scalar.activation(cs2_col[:], cs_col[:], SQUARE)
         nc.gpsimd.memset(window[2][:], 0.0)
-        for t in range(4):
-            nc.tensor.transpose(banks[7][:, t * P : (t + 1) * P], cs2_col[:, t : t + 1].to_broadcast([P, P]), ident[:])
-        zT_in = tile("zT_in", 4 * R, BF16)[:]
-        xm_dealt = tile("xm_dealt", 4 * D, F32)[:]
-        picked = tile("picked", 4 * N, BF16)[:]
-        zm_in = [tile("zm_in%d" % h, 2 * N, BF16)[:] for h in range(2)]
-        wi01_in = zT_raw[:, 0:N].bitcast(BF16)
-        wi23_in = xm_raw[:, 0:N].bitcast(BF16)
-        wi_in = [wi01_in[:, 0:N], wi01_in[:, N : 2 * N], wi23_in[:, 0:N], wi23_in[:, N : 2 * N]]
-        resid = [tile("resid%d" % t, D, F32)[:] for t in range(4)]
-        e_pair = [tile("e_pair%d" % k, 2 * D, BF16)[:] for k in range(2)]
-        e_r = [e_pair[t // 2][:, (t % 2) * D : (t % 2 + 1) * D] for t in range(4)]
-        dw = [tile("dw%d" % t, N, F32)[:] for t in range(4)]
-        wd_in = zm_raw[1][:].bitcast(BF16)
-        ed_both = tile("ed_both", 4 * R, BF16)[:]
-        ed_in = [ed_both[:, u * 2 * R : (u + 1) * 2 * R] for u in range(2)]
-        w_bank = [0, 6, 0, 6]
-        rec_bank = [1, 2, 3, 7]
-        e_bank = [4, 5]
-        dw_bank = [1, 4, 5, 0]
-        gz_bank = [0, 2, 3, 7]
-        q = {}
-
-        def lay_zT(engine_copy, lo, hi):
-            engine_copy(
-                zT_in.rearrange("p (a m j) -> p m j a", a=4, j=4)[:, lo:hi],
-                zT_raw[:].rearrange("p (j m a) -> p m j a", j=4, a=4)[:, lo:hi],
-            )
-
-        def lay_xm(engine_copy, lo, hi):
-            engine_copy(
-                xm_dealt.rearrange("p (t q j) -> p q j t", t=4, j=4)[:, lo:hi],
-                xm_raw[:].rearrange("p (j q t) -> p q j t", j=4, t=4)[:, lo:hi],
-            )
-
-        def lay_zm(engine_copy, h):
-            engine_copy(
-                zm_in[h].rearrange("p (c i j) -> p c j i", i=4, j=4),
-                zm_raw[h][:].rearrange("p (j c i) -> p c j i", j=4, i=4),
-            )
-
-        zm_q = (tile("zm_codes", N, U32), tile("zm_scales", N, U8))
-
-        def quantize_zm(h):
-            cols = slice(h * 256, (h + 1) * 256)
-            nc.vector.quantize_mx(out=zm_q[0][:, cols].bitcast(E4), scales=zm_q[1][:, cols], in_=zm_in[h])
-
-        def gather(t):
-            nc.vector.tensor_copy(picked[:, t * N : (t + 1) * N], table[t][:].indirect(offsets[:]))
-
-        def turn_w(t, engine_copy=nc.scalar.copy):
-            words = picked[:, t * N : (t + 1) * N].bitcast(F32)
-            turned = banks[w_bank[t]]
-            for u in range(2):
-                nc.tensor.transpose(turned[:, u * P : (u + 1) * P], words[:, u : 2 * P : 2], ident[:])
-            engine_copy(
-                wi_in[t].bitcast(F32).rearrange("p (q u) -> p q u", u=2),
-                turned[:, 0 : 2 * P].rearrange("p (u q) -> p q u", u=2),
-            )
-
-        def quantize_w(t):
-            q["wi", t] = quantize("wi%d" % t, wi_in[t], E4)
-
-        def quantize_w01():
-            codes, scales = quantize("wi01", wi01_in, E4)
-            for t in range(2):
-                q["wi", t] = (codes[:, t * P : (t + 1) * P], scales[:, t * P : (t + 1) * P])
-
-        def quantize_w23():
-            codes, scales = quantize("wi23", wi23_in, E4)
-            for t in range(2):
-                q["wi", 2 + t] = (codes[:, t * P : (t + 1) * P], scales[:, t * P : (t + 1) * P])
-
-        def reconstruct(t):
-            wi_q = q["wi", t]
-            for a in range(4):
-                cols = slice(a * P, (a + 1) * P)
-                product(banks[rec_bank[t]][:, cols], q["zT"], E4, cols, wi_q)
-
-        def residual(t):
-            nc.vector.tensor_tensor(
-                resid[t].rearrange("p (q a) -> p q a", a=4),
-                banks[rec_bank[t]][:].rearrange("p (a q) -> p q a", a=4),
-                xm_dealt[:, t * D : (t + 1) * D].rearrange("p (q a) -> p q a", a=4),
-                SUB,
-            )
-
-        def weigh(t, engine=nc.vector):
-            engine.tensor_tensor(e_r[t], resid[t], gain[:, t * D : (t + 1) * D], MULT)
-
-        def quantize_e(t):
-            q["e", t] = quantize("er%d" % t, e_r[t], E5)
-
-        def quantize_e_pair(k):
-            codes, scales = quantize("er_pair%d" % k, e_pair[k], E5)
-            for t in range(2):
-                q["e", 2 * k + t] = (codes[:, t * P : (t + 1) * P], scales[:, t * P : (t + 1) * P])
-
-        def quantize_ed_both():
-            codes, scales = quantize("ed", ed_both, E5)
-            for u in range(2):
-                q["ed", u] = (codes[:, u * 256 : (u + 1) * 256], scales[:, u * 256 : (u + 1) * 256])
-
-        def turn_e(t):
-            words = e_r[t].bitcast(F32)
-            for u in range(2):
-                nc.tensor.transpose(banks[e_bank[u]][:, t * P : (t + 1) * P], words[:, u : 2 * P : 2], ident[:])
-
-        def atoms_product(t):
-            product(banks[dw_bank[t]][:], q["e", t], E5, slice(0, P), zm_q)
-
-        def leave(t, lo, hi):
-            nc.scalar.copy(dw[t][:, lo:hi], banks[dw_bank[t]][:, lo:hi])
-
-        def scatter(t, lo, hi):
-            win = window[t % len(window)]
-            nc.vector.tensor_copy(win[:].indirect(offsets[:, lo // 16 : hi // 16]), dw[t][:, lo:hi])
-            if hi == N:
-                nc.sync.dma_start(out0_planes[:, t, :], win[:])
-
-        def lay_wd(k):
-            nc.scalar.copy(
-                wd_in[:, k * N : (k + 1) * N].rearrange("p (c i t) -> p c t i", i=4, t=4),
-                picked.rearrange("p (t c i) -> p c t i", t=4, i=4)[:, k * 32 : (k + 1) * 32],
-            )
-
-        def lay_ed(u):
-            nc.scalar.copy(
-                ed_in[u].rearrange("q (e p t) -> q e p t", e=2, t=4),
-                banks[e_bank[u]][:].bitcast(BF16).rearrange("q (t p e) -> q e p t", t=4, e=2),
-            )
-
-        def quantize_ed(u):
-            q["ed", u] = quantize("ed%d" % u, ed_in[u], E5)
-
-        def codes_gradient(u):
-            gz = tile("gz%d" % u, 2 * N, F32)
-            for e in range(2):
-                acc = banks[gz_bank[2 * u + e]]
-                product(acc[:], q["ed", u], E5, slice(e * P, (e + 1) * P), q["wd"])
-                nc.scalar.copy(gz[:, e * N : (e + 1) * N], acc[:])
-            nc.scalar.dma_start(out1_rows[:, 2 * u : 2 * u + 2, :], gz[:].rearrange("p (e i) -> p e i", e=2))
-
-        gain = tile("gain", 4 * D, F32, tag="gain")
+        for t in range(PACK):
+            nc.tensor.transpose(part(cs2_bank, t, P), cs2_col[:, t : t + 1].to_broadcast([P, P]), ident[:])
+        gain = tile("gain", PACK * D, F32)
         nc.vector.tensor_tensor(
-            gain[:].rearrange("p (c j) -> p c j", j=4),
-            banks[7][:].unsqueeze(2).to_broadcast([P, D, 4]),
-            wt_col[:].unsqueeze(1).to_broadcast([P, D, 4]),
+            gain[:].rearrange("m (c a) -> m c a", a=PACK),
+            cs2_bank[:].unsqueeze(2).to_broadcast([P, D, PACK]),
+            wt_col[:].unsqueeze(1).to_broadcast([P, D, PACK]),
             MULT,
         )
 
+        picked = tile("picked", PACK * N, BF16)[:]
+        zT_laid = tile("zT_laid", PACK * R, BF16)[:]
+        xm_laid = tile("xm_laid", PACK * D, F32)[:]
+        zm_laid = [tile("zm_laid%d" % h, 2 * N, BF16)[:] for h in range(2)]
+        w_pair = [raw[:, 0:N].bitcast(BF16) for raw in (zT_raw, xm_raw)]
+        w_along_i = [part(w_pair[t // 2], t % 2, N) for t in range(PACK)]
+        w_along_d = zm_raw[:, 0 : 2 * N].bitcast(BF16)
+        resid = [tile("resid0", D, F32)[:], tile("resid1", D, F32)[:], part(zm_raw, 2, N), part(zm_raw, 3, N)]
+        e_pair = [tile("e_pair%d" % k, 2 * D, BF16)[:] for k in range(2)]
+        e_along_r = [part(e_pair[t // 2], t % 2, D) for t in range(PACK)]
+        e_along_d = tile("e_along_d", PACK * R, BF16)[:]
+        zm_mx = (tile("zm_words", N, U32)[:], tile("zm_scales", N, U8)[:])
+
+        def lay_out(dst, src):
+            nc.vector.tensor_copy(dst[:, 0:VECTOR_SHARE], src[:, 0:VECTOR_SHARE])
+            nc.scalar.copy(dst[:, VECTOR_SHARE:P], src[:, VECTOR_SHARE:P])
+
+        def gather(t):
+            nc.vector.tensor_copy(part(picked, t, N), table[t][:].indirect(offsets[:]))
+
+        def turn_pairs(values, targets):
+            words = values.bitcast(F32)
+            for u in range(2):
+                nc.tensor.transpose(targets[u], words[:, u : 2 * P : 2], ident[:])
+
+        def turn_w(t):
+            bank = w_turn_bank[t]
+            turn_pairs(part(picked, t, N), [part(bank, u, P) for u in range(2)])
+            nc.scalar.copy(
+                w_along_i[t].bitcast(F32).rearrange("p (q u) -> p q u", u=2),
+                bank[:, 0 : 2 * P].rearrange("p (u q) -> p q u", u=2),
+            )
+
+        def reconstruct(k, zT_mx):
+            w_mx = quantize("w_pair%d" % k, w_pair[k], E4M3)
+            for j in range(2):
+                for a in range(PACK):
+                    product(part(rec_bank[2 * k + j], a, P), columns(zT_mx, a, P), E4M3, columns(w_mx, j, P))
+
+        def error(k):
+            planes = (2 * k, 2 * k + 1)
+            for t in planes:
+                nc.vector.tensor_tensor(
+                    resid[t].rearrange("m (q a) -> m q a", a=PACK),
+                    rec_bank[t][:].rearrange("m (a q) -> m q a", a=PACK),
+                    part(xm_laid, t, D).rearrange("m (q a) -> m q a", a=PACK),
+                    SUBTRACT,
+                )
+            for t in planes:
+                nc.vector.tensor_tensor(e_along_r[t], resid[t], part(gain, t, D), MULT)
+            e_mx = quantize("e_pair%d" % k, e_pair[k], E5M2)
+            for t in planes:
+                turn_pairs(e_along_r[t], [part(e_turn_bank[u], t, P) for u in range(2)])
+            return [columns(e_mx, j, P) for j in range(2)]
+
+        def atoms_gradient(t, e_mx):
+            product(dw_bank[t][:], e_mx, E5M2, zm_mx)
+            dw = tile("dw%d" % t, N, F32)
+            nc.scalar.copy(dw[:], dw_bank[t][:])
+            target = window[t % len(window)]
+            nc.vector.tensor_copy(target[:].indirect(offsets[:]), dw[:])
+            nc.sync.dma_start(out_0_planes[:, t, :], target[:])
+
+        def coefficients_gradient(u, e_mx, w_mx):
+            dz = tile("dz%d" % u, 2 * N, F32)
+            for j in range(2):
+                a = 2 * u + j
+                product(dz_bank[a][:], columns(e_mx, a, P), E5M2, w_mx)
+                nc.scalar.copy(part(dz, j, N), dz_bank[a][:])
+            nc.scalar.dma_start(out_1_rows[:, 2 * u : 2 * u + 2, :], dz[:].rearrange("m (j i) -> m j i", j=2))
+
         gather(0)
         gather(1)
-        lay_zT(nc.vector.tensor_copy, 0, 80)
-        lay_zT(nc.scalar.copy, 80, 128)
+        lay_out(
+            zT_laid.rearrange("p (a m s) -> p m s a", a=PACK, s=PACK),
+            zT_raw[:].rearrange("p (s m a) -> p m s a", s=PACK, a=PACK),
+        )
         turn_w(0)
         turn_w(1)
-        q["zT"] = quantize("zT", zT_in, E4)
-        quantize_w01()
-        reconstruct(0)
-        reconstruct(1)
+        zT_mx = quantize("zT", zT_laid, E4M3)
+        reconstruct(0, zT_mx)
+
         gather(2)
         gather(3)
-        lay_xm(nc.vector.tensor_copy, 0, 80)
-        lay_xm(nc.scalar.copy, 80, 128)
+        lay_out(
+            xm_laid.rearrange("m (t q a) -> m q a t", t=PACK, a=PACK),
+            xm_raw[:].rearrange("m (a q t) -> m q a t", a=PACK, t=PACK),
+        )
         turn_w(2)
         turn_w(3)
-        quantize_w23()
-        reconstruct(2)
-        reconstruct(3)
-        lay_zm(nc.scalar.copy, 0)
-        quantize_zm(0)
-        lay_zm(nc.scalar.copy, 1)
-        quantize_zm(1)
-        residual(0)
-        residual(1)
-        weigh(0)
-        weigh(1)
-        quantize_e_pair(0)
-        turn_e(0)
-        turn_e(1)
-        residual(2)
-        residual(3)
-        weigh(2)
-        weigh(3)
-        quantize_e_pair(1)
-        turn_e(2)
-        turn_e(3)
-        atoms_product(0)
-        leave(0, 0, 512)
-        scatter(0, 0, 512)
-        lay_wd(0)
-        lay_wd(1)
-        lay_wd(2)
-        lay_wd(3)
-        q["wd"] = quantize("wd", wd_in, E4)
-        lay_ed(0)
-        lay_ed(1)
-        quantize_ed_both()
-        atoms_product(1)
-        leave(1, 0, 512)
-        scatter(1, 0, 512)
-        codes_gradient(0)
-        atoms_product(2)
-        leave(2, 0, 512)
-        scatter(2, 0, 512)
-        codes_gradient(1)
-        atoms_product(3)
-        leave(3, 0, 512)
-        scatter(3, 0, 512)
+        reconstruct(1, zT_mx)
+
+        zm_groups = zm_raw[:].rearrange("m (a c i) -> m c a i", a=PACK, i=4)
+        for h in range(2):
+            nc.scalar.copy(zm_laid[h].rearrange("m (c i a) -> m c a i", i=4, a=PACK), part(zm_groups, h, N // 8))
+            words, scales = columns(zm_mx, h, N // 2)
+            nc.vector.quantize_mx(out=words.bitcast(E4M3), scales=scales, in_=zm_laid[h])
+
+        e_along_r_mx = error(0) + error(1)
+        atoms_gradient(0, e_along_r_mx[0])
+
+        w_groups = picked.rearrange("q (t c i) -> q c t i", t=PACK, i=4)
+        for j in range(4):
+            nc.scalar.copy(part(w_along_d, j, N).rearrange("q (c i t) -> q c t i", i=4, t=PACK), part(w_groups, j, N // 16))
+        w_along_d_mx = quantize("w_along_d", w_along_d, E4M3)
+        for u in range(2):
+            nc.scalar.copy(
+                part(e_along_d, u, 2 * R).rearrange("q (j m t) -> q j m t", j=2, t=PACK),
+                e_turn_bank[u][:].bitcast(BF16).rearrange("q (t m j) -> q j m t", t=PACK, j=2),
+            )
+        e_along_d_mx = quantize("e_along_d", e_along_d, E5M2)
+
+        atoms_gradient(1, e_along_r_mx[1])
+        coefficients_gradient(0, e_along_d_mx, w_along_d_mx)
+        atoms_gradient(2, e_along_r_mx[2])
+        coefficients_gradient(1, e_along_d_mx, w_along_d_mx)
+        atoms_gradient(3, e_along_r_mx[3])

from contextlib import ExitStack

import concourse.mybir as mybir

N, T, D, R = 512, 2048, 512, 512
P = 128
PACK = 4
FLOPS = 3 * 2 * N * D * R

VECTOR_SHARE = 80

F32 = mybir.dt.float32
BF16 = mybir.dt.bfloat16
U32 = mybir.dt.uint32
U16 = mybir.dt.uint16
U8 = mybir.dt.uint8
E4M3 = mybir.dt.float8_e4m3fn_x4
E5M2 = mybir.dt.float8_e5m2_x4
MULT = mybir.AluOpType.mult
SUBTRACT = mybir.AluOpType.subtract
SQUARE = mybir.ActivationFunctionType.Square


def tile_attend_gdi_wz_kernel(tc, zT, wT, xm, wt, zm, cs, offs, out_0, out_1):
    nc = tc.nc
    with ExitStack() as ctx:
        lists = ctx.enter_context(tc.tile_pool(name="lists", bufs=1))
        sb = ctx.enter_context(tc.tile_pool(name="sb", bufs=1))
        ps = ctx.enter_context(tc.psum_pool(name="ps", bufs=1))

        def tile(name, width, dtype, tag=""):
            return sb.tile([P, width], dtype, name=name, tag=tag or name, align_bytes=64)

        def part(ap, index, width):
            return ap[:, index * width : (index + 1) * width]

        def quantize(name, values, fmt):
            words = tile(name + "_words", values.shape[1] // PACK, U32)
            scales = tile(name + "_scales", values.shape[1] // PACK, U8)
            nc.vector.quantize_mx(out=words[:].bitcast(fmt), scales=scales[:], in_=values)
            return words[:], scales[:]

        def columns(operand, index, width):
            return part(operand[0], index, width), part(operand[1], index, width)

        def product(acc, stationary, stationary_fmt, moving):
            nc.tensor.matmul_mx(
                acc,
                lhsT=stationary[0].bitcast(stationary_fmt),
                lhsT_scale=stationary[1],
                rhs=moving[0].bitcast(E4M3),
                rhs_scale=moving[1],
                start=True,
                stop=True,
            )

        banks = [ps.tile([P, 512], F32, name="bank%d" % b) for b in range(8)]
        cs2_bank = banks[7]
        w_turn_bank = [banks[0], banks[6], banks[0], banks[6]]
        rec_bank = [banks[1], banks[2], banks[3], banks[7]]
        e_turn_bank = [banks[4], banks[5]]
        dw_bank = [banks[1], banks[4], banks[5], banks[0]]
        dz_bank = [banks[0], banks[2], banks[3], banks[7]]

        offsets = lists.tile([P, N // 16], U16, name="offsets")
        cs_col = tile("cs_col", PACK, F32)
        wt_col = tile("wt_col", PACK, F32)
        zT_raw = tile("zT_raw", PACK * R, F32)
        xm_raw = tile("xm_raw", PACK * D, F32)
        zm_raw = tile("zm_raw", PACK * N, F32)
        table = [tile("table%d" % t, T, F32) for t in range(PACK)]
        wT_planes = wT.rearrange("(q t) c -> q t c", t=PACK)
        out_0_planes = out_0.rearrange("(q t) c -> q t c", t=PACK)
        out_1_rows = out_1[0].rearrange("(m a) i -> m a i", a=PACK)

        nc.sync.dma_start(cs_col[:], cs[0:1, :].rearrange("o (q t) -> (o q) t", t=PACK))
        nc.sync.dma_start(wt_col[:], wt[0].rearrange("(m a) o -> m (a o)", a=PACK))
        nc.sync.dma_start(table[0][:], wT_planes[:, 0, :])
        nc.sync.dma_start(offsets[:], offs)
        nc.sync.dma_start(table[1][:], wT_planes[:, 1, :])
        nc.sync.dma_start(zT_raw[:], zT[0].rearrange("(p s) r -> p (s r)", s=PACK))
        nc.sync.dma_start(table[2][:], wT_planes[:, 2, :])
        nc.sync.dma_start(table[3][:], wT_planes[:, 3, :])
        nc.sync.dma_start(xm_raw[:], xm[0].rearrange("(m a) d -> m (a d)", a=PACK))
        nc.sync.dma_start(zm_raw[:], zm[0].rearrange("(m a) i -> m (a i)", a=PACK))

        ident = tile("ident", P, F32)
        zeros = tile("zeros", P, F32, tag="window1")
        nc.vector.memset(zeros[:], 0.0)
        nc.gpsimd.affine_select(
            out=ident[:],
            in_=zeros[:],
            compare_op=mybir.AluOpType.not_equal,
            fill=1.0,
            base=0,
            pattern=[[-1, P]],
            channel_multiplier=1,
        )
        window = [tile("window0", T, F32), tile("window1", T, F32), tile("window2", T, F32, tag="cs_col")]
        nc.vector.memset(window[0][:], 0.0)
        nc.gpsimd.memset(window[1][:], 0.0)

        cs2_col = tile("cs2_col", PACK, F32)
        nc.scalar.activation(cs2_col[:], cs_col[:], SQUARE)
        nc.gpsimd.memset(window[2][:], 0.0)
        for t in range(PACK):
            nc.tensor.transpose(part(cs2_bank, t, P), cs2_col[:, t : t + 1].to_broadcast([P, P]), ident[:])
        gain = tile("gain", PACK * D, F32)
        nc.vector.tensor_tensor(
            gain[:].rearrange("m (c a) -> m c a", a=PACK),
            cs2_bank[:].unsqueeze(2).to_broadcast([P, D, PACK]),
            wt_col[:].unsqueeze(1).to_broadcast([P, D, PACK]),
            MULT,
        )

        picked = tile("picked", PACK * N, BF16)[:]
        zT_laid = tile("zT_laid", PACK * R, BF16)[:]
        xm_laid = tile("xm_laid", PACK * D, F32)[:]
        zm_laid = [tile("zm_laid%d" % h, 2 * N, BF16)[:] for h in range(2)]
        w_pair = [raw[:, 0:N].bitcast(BF16) for raw in (zT_raw, xm_raw)]
        w_along_i = [part(w_pair[t // 2], t % 2, N) for t in range(PACK)]
        w_along_d = zm_raw[:, 0 : 2 * N].bitcast(BF16)
        resid = [tile("resid0", D, F32)[:], tile("resid1", D, F32)[:], part(zm_raw, 2, N), part(zm_raw, 3, N)]
        e_pair = [tile("e_pair%d" % k, 2 * D, BF16)[:] for k in range(2)]
        e_along_r = [part(e_pair[t // 2], t % 2, D) for t in range(PACK)]
        e_along_d = tile("e_along_d", PACK * R, BF16)[:]
        zm_mx = (tile("zm_words", N, U32)[:], tile("zm_scales", N, U8)[:])

        def lay_out(dst, src):
            nc.vector.tensor_copy(dst[:, 0:VECTOR_SHARE], src[:, 0:VECTOR_SHARE])
            nc.scalar.copy(dst[:, VECTOR_SHARE:P], src[:, VECTOR_SHARE:P])

        def gather(t):
            nc.vector.tensor_copy(part(picked, t, N), table[t][:].indirect(offsets[:]))

        def turn_pairs(values, targets):
            words = values.bitcast(F32)
            for u in range(2):
                nc.tensor.transpose(targets[u], words[:, u : 2 * P : 2], ident[:])

        def turn_w(t):
            bank = w_turn_bank[t]
            turn_pairs(part(picked, t, N), [part(bank, u, P) for u in range(2)])
            nc.scalar.copy(
                w_along_i[t].bitcast(F32).rearrange("p (q u) -> p q u", u=2),
                bank[:, 0 : 2 * P].rearrange("p (u q) -> p q u", u=2),
            )

        def reconstruct(k, zT_mx):
            w_mx = quantize("w_pair%d" % k, w_pair[k], E4M3)
            for j in range(2):
                for a in range(PACK):
                    product(part(rec_bank[2 * k + j], a, P), columns(zT_mx, a, P), E4M3, columns(w_mx, j, P))

        def error(k):
            planes = (2 * k, 2 * k + 1)
            for t in planes:
                nc.vector.tensor_tensor(
                    resid[t].rearrange("m (q a) -> m q a", a=PACK),
                    rec_bank[t][:].rearrange("m (a q) -> m q a", a=PACK),
                    part(xm_laid, t, D).rearrange("m (q a) -> m q a", a=PACK),
                    SUBTRACT,
                )
            for t in planes:
                nc.vector.tensor_tensor(e_along_r[t], resid[t], part(gain, t, D), MULT)
            e_mx = quantize("e_pair%d" % k, e_pair[k], E5M2)
            for t in planes:
                turn_pairs(e_along_r[t], [part(e_turn_bank[u], t, P) for u in range(2)])
            return [columns(e_mx, j, P) for j in range(2)]

        def atoms_gradient(t, e_mx):
            product(dw_bank[t][:], e_mx, E5M2, zm_mx)
            dw = tile("dw%d" % t, N, F32)
            nc.scalar.copy(dw[:], dw_bank[t][:])
            target = window[t % len(window)]
            nc.vector.tensor_copy(target[:].indirect(offsets[:]), dw[:])
            nc.sync.dma_start(out_0_planes[:, t, :], target[:])

        def coefficients_gradient(u, e_mx, w_mx):
            dz = tile("dz%d" % u, 2 * N, F32)
            for j in range(2):
                a = 2 * u + j
                product(dz_bank[a][:], columns(e_mx, a, P), E5M2, w_mx)
                nc.scalar.copy(part(dz, j, N), dz_bank[a][:])
            nc.scalar.dma_start(out_1_rows[:, 2 * u : 2 * u + 2, :], dz[:].rearrange("m (j i) -> m j i", j=2))

        gather(0)
        gather(1)
        lay_out(
            zT_laid.rearrange("p (a m s) -> p m s a", a=PACK, s=PACK),
            zT_raw[:].rearrange("p (s m a) -> p m s a", s=PACK, a=PACK),
        )
        turn_w(0)
        turn_w(1)
        zT_mx = quantize("zT", zT_laid, E4M3)
        reconstruct(0, zT_mx)

        gather(2)
        gather(3)
        lay_out(
            xm_laid.rearrange("m (t q a) -> m q a t", t=PACK, a=PACK),
            xm_raw[:].rearrange("m (a q t) -> m q a t", a=PACK, t=PACK),
        )
        turn_w(2)
        turn_w(3)
        reconstruct(1, zT_mx)

        zm_groups = zm_raw[:].rearrange("m (a c i) -> m c a i", a=PACK, i=4)
        for h in range(2):
            nc.scalar.copy(zm_laid[h].rearrange("m (c i a) -> m c a i", i=4, a=PACK), part(zm_groups, h, N // 8))
            words, scales = columns(zm_mx, h, N // 2)
            nc.vector.quantize_mx(out=words.bitcast(E4M3), scales=scales, in_=zm_laid[h])

        e_along_r_mx = error(0) + error(1)
        atoms_gradient(0, e_along_r_mx[0])

        w_groups = picked.rearrange("q (t c i) -> q c t i", t=PACK, i=4)
        for j in range(4):
            nc.scalar.copy(part(w_along_d, j, N).rearrange("q (c i t) -> q c t i", i=4, t=PACK), part(w_groups, j, N // 16))
        w_along_d_mx = quantize("w_along_d", w_along_d, E4M3)
        for u in range(2):
            nc.scalar.copy(
                part(e_along_d, u, 2 * R).rearrange("q (j m t) -> q j m t", j=2, t=PACK),
                e_turn_bank[u][:].bitcast(BF16).rearrange("q (t m j) -> q j m t", t=PACK, j=2),
            )
        e_along_d_mx = quantize("e_along_d", e_along_d, E5M2)

        atoms_gradient(1, e_along_r_mx[1])
        coefficients_gradient(0, e_along_d_mx, w_along_d_mx)
        atoms_gradient(2, e_along_r_mx[2])
        coefficients_gradient(1, e_along_d_mx, w_along_d_mx)
        atoms_gradient(3, e_along_r_mx[3])
